import numpy as np
import ml_dtypes


def mxq(x, axis, fmt="e4m3"):
    dtype, down = {"e4m3": (ml_dtypes.float8_e4m3fn, 7), "e5m2": (ml_dtypes.float8_e5m2, 14)}[fmt]
    v = np.moveaxis(np.asarray(x, np.float32).astype(ml_dtypes.bfloat16).astype(np.float64), axis, -1)
    blocks = v.reshape(v.shape[:-1] + (-1, 32))
    amax = np.abs(blocks).max(-1, keepdims=True)
    byte = np.maximum(np.where(amax > 0, np.frexp(amax)[1] - 1 + 127, 0) - down, 1)
    scale = np.exp2(byte - 127.0)
    codes = (blocks / scale).astype(np.float32).astype(dtype).astype(np.float64)
    return np.moveaxis((codes * scale).reshape(v.shape), -1, axis)


WIDE = False


def mx_kscale(k):
    if not WIDE:
        return np.ones(k)
    levels = np.array([10, -10, 5, -5, 0])
    if k % 512:
        return np.exp2(np.random.permutation(np.resize(levels, k // 32))).repeat(32)
    a = np.empty((k // 512, 16))
    for p in range(k // 512):
        a[p, :8] = np.random.permutation(np.resize(levels, 8))
        for g in range(8):
            far = levels[np.abs(levels - a[p, g]) >= 10]
            a[p, g + 8] = far[np.random.randint(len(far))]
    return np.exp2(a.ravel()).repeat(32)


def f64(x):
    return np.asarray(x).astype(np.float64)


def striped(idx):
    return np.tile(idx.reshape(-1, 16).T, (8, 1)).astype(np.uint16)


def unstriped(offs):
    return offs[:16].T.reshape(-1).astype(np.int64)


E2M1 = np.array([0.0, 0.5, 1.0, 1.5, 2.0, 3.0, 4.0, 6.0, -0.0, -0.5, -1.0, -1.5, -2.0, -3.0, -4.0, -6.0])


def pack_weight(w, fmt):
    k, n = w.shape
    w = f64(np.asarray(w, np.float32).astype(ml_dtypes.bfloat16)).reshape(k // 32, 32, n)
    amax = np.abs(w).max(1)
    if fmt == "e4m3":
        byte = np.frexp(amax)[1] - 1 + 127 - 7
    else:
        mant, ex = np.frexp(amax / 6.0)
        byte = np.where(mant > 0.5, ex, ex - 1) + 127
    byte = np.clip(np.where(amax > 0, byte, 1), 1, 254)
    scaled = (w * np.exp2(127.0 - byte)[:, None, :]).reshape(k, n).astype(np.float32)
    by_word = np.ascontiguousarray(scaled.reshape(k // 512, 128, 4, n).transpose(0, 1, 3, 2))
    if fmt == "e4m3":
        words = by_word.astype(ml_dtypes.float8_e4m3fn).view(np.uint8)
    else:
        c = by_word.astype(ml_dtypes.float4_e2m1fn).view(np.uint8) & 0xF
        words = (c[..., 0::2] | (c[..., 1::2] << 4)).reshape(k // 512, 128, 2 * n)
    return np.ascontiguousarray(words), np.ascontiguousarray(byte.astype(np.uint8).reshape(k // 512, 16, n))


def unpack_weight(words, scales, fmt):
    g, _, n = scales.shape
    words = np.ascontiguousarray(words).reshape(g, 128, n, -1)
    if fmt == "e4m3":
        vals = words.view(ml_dtypes.float8_e4m3fn).astype(np.float64)
    else:
        nib = np.empty((g, 128, n, 4), np.uint8)
        nib[..., 0::2] = words & 0xF
        nib[..., 1::2] = words >> 4
        vals = E2M1[nib]
    vals = vals * np.repeat(np.exp2(scales.astype(np.float64) - 127.0), 8, axis=1)[..., None]
    return vals.transpose(0, 1, 3, 2).reshape(g * 512, n)


def relu2(v):
    return np.maximum(v, 0.0) ** 2


K, T, E, C, H, N = 2048, 640, 5, 256, 512, 256


def by_expert(wq, xq):
    return np.concatenate([wq[e].T @ xq[:, e * C:(e + 1) * C] for e in range(E)], axis=1)


def setup_inputs():
    n = np.random.standard_normal
    s = mx_kscale(K)[:, None]
    u = mx_kscale(H)
    first = np.random.permutation(np.repeat(np.arange(E), T // E))
    second = (first + 1 + np.random.permutation(np.repeat(np.arange(E - 1), -(-T // (E - 1)))[:T])) % E
    while np.bincount(second, minlength=E).max() != T // E:
        load = np.bincount(second, minlength=E); hi, lo = int(load.argmax()), int(load.argmin())
        t = np.flatnonzero((second == hi) & (first != lo))[0]; second[t] = lo
    slot_token = np.empty(E * C, np.int64); pos = np.empty((2, T), np.int64); fill = np.zeros(E, np.int64)
    place = np.stack([np.random.permutation(C) for _ in range(E)])
    for r, deal in enumerate((first, second)):
        for t in np.random.permutation(T):
            e = deal[t]; j = e * C + place[e, fill[e]]; fill[e] += 1; slot_token[j] = t; pos[r, t] = j
    g = np.random.uniform(0.2, 0.8, T)
    w1 = [pack_weight(m, "e2m1") for m in n((E, K, H)) / np.sqrt(K) / s[None] * u[None, None, :]]
    w2 = [pack_weight(m, "e2m1") for m in n((E, H, N)) / np.sqrt(H) / u[None, :, None] ** 2]
    x = pack_weight(n((K, T)) * s, "e4m3")
    return {
        "x_words": x[0],
        "x_scales": x[1],
        "w1_words": np.stack([m[0] for m in w1]),
        "w1_scales": np.stack([m[1] for m in w1]),
        "w2_words": np.stack([m[0] for m in w2]),
        "w2_scales": np.stack([m[1] for m in w2]),
        "gate": np.stack([np.tile(g, (N, 1)), np.tile(1.0 - g, (N, 1))]).astype(np.float32),
        "offs": striped(slot_token),
        "pos1": striped(pos[0]),
        "pos2": striped(pos[1]),
    }


def reference(x_words, x_scales, w1_words, w1_scales, w2_words, w2_scales, gate, offs, pos1, pos2):
    idx = unstriped(offs)
    w1 = np.stack([unpack_weight(w1_words[e], w1_scales[e], "e2m1") for e in range(E)])
    w2 = np.stack([unpack_weight(w2_words[e], w2_scales[e], "e2m1") for e in range(E)])
    xq = unpack_weight(x_words, x_scales, "e4m3")[:, idx]
    h = relu2(by_expert(w1, xq))
    y = by_expert(w2, mxq(h, 0, "e4m3"))
    return f64(gate[0]) * y[:, unstriped(pos1)] + f64(gate[1]) * y[:, unstriped(pos2)]

@@ -1,0 +1,282 @@
+from contextlib import ExitStack
+
+import concourse.mybir as mybir
+from concourse.masks import make_identity
+
+K, T, E, C, H, N = 2048, 640, 5, 256, 512, 256
+FLOPS = 2 * E * C * (K * H + H * N)
+
+F32 = mybir.dt.float32
+BF16 = mybir.dt.bfloat16
+I32 = mybir.dt.int32
+U32 = mybir.dt.uint32
+U16 = mybir.dt.uint16
+U8 = mybir.dt.uint8
+FP8X4 = mybir.dt.float8_e4m3fn_x4
+FP4X4 = mybir.dt.float4_e2m1fn_x4
+ACT = mybir.ActivationFunctionType
+ALU = mybir.AluOpType
+
+P = 128
+PASSES = K // 512
+S = E * C
+BLOCKS = S // P
+W1_BYTES = PASSES * 2 * H
+W1_SCALE_BYTES = PASSES * H
+W2_BYTES = 2 * N
+SCALE_WINDOW = 1024
+FIRST_SLOTS = 2 * C
+SHIFT_ROWS = 112
+
+
+def tile_moe_pkd_mlp_relu2_kernel(
+    tc, x_words, x_scales, w1_words, w1_scales, w2_words, w2_scales, gate, offs, pos1, pos2, out
+):
+    nc = tc.nc
+    with ExitStack() as ctx:
+        lists = ctx.enter_context(tc.tile_pool(name="lists", bufs=1))
+        keep = ctx.enter_context(tc.tile_pool(name="keep", bufs=1))
+        ring = ctx.enter_context(tc.tile_pool(name="ring", bufs=2))
+        work = ctx.enter_context(tc.tile_pool(name="work", bufs=4))
+        psum = ctx.enter_context(tc.psum_pool(name="psum", bufs=1))
+
+        def bank(index, shape):
+            return psum.tile(shape, F32, name="bank%d" % index)
+
+        offs_sb = lists.tile([P, S // 16], U16, name="offs_sb")
+        pos_sb = [lists.tile([P, T // 16], U16, name="pos%d_sb" % r) for r in range(2)]
+        nc.sync.dma_start(offs_sb[:], offs)
+
+        xs_window = keep.tile([P, SCALE_WINDOW], U8, name="xs_window", align_bytes=64)
+        nc.vector.memset(xs_window[:].bitcast(I32), 0)
+
+        for q in range(4):
+            queue = nc.sync if q < 2 else nc.scalar
+            queue.dma_start(
+                xs_window[32 * q : 32 * q + 16, 0:T].bitcast(I32),
+                x_scales[:, 4 * q : 4 * q + 4, :].bitcast(I32),
+            )
+        xw = keep.tile([P, PASSES * T], I32, name="xw", align_bytes=64)
+        nc.sync.dma_start(
+            xw[:].rearrange("p (a t) -> p a t", a=PASSES),
+            x_words.rearrange("a p t r -> p a (t r)").bitcast(I32),
+        )
+
+        w1_planes = {}
+
+        def load_w1_scales(e0, e1, queue, zeroing):
+            planes = keep.tile([P, (e1 - e0) * W1_SCALE_BYTES], U8, name="w1_planes%d" % e0, align_bytes=64)
+            zeroing.memset(planes[:].bitcast(I32), 0)
+            for e in range(e0, e1):
+                w1_planes[e] = planes[:, (e - e0) * W1_SCALE_BYTES : (e - e0 + 1) * W1_SCALE_BYTES]
+            src = w1_scales[e0:e1].rearrange("e s (q r) i -> r q (e s) i", r=4)
+            for r in range(4):
+                dst = planes[r:P:32, :].bitcast(I32).rearrange("q (g i) -> q g i", i=H // 4)
+                queue.dma_start(dst, src[r].bitcast(I32))
+
+        w1_sb = [keep.tile([P, W1_BYTES], U8, name="w1_%d" % i, align_bytes=64) for i in range(E)]
+
+        def load_w1(e):
+            dst = w1_sb[e][:].bitcast(I32).rearrange("p (s b) -> p s b", s=PASSES)
+            nc.sync.dma_start(dst, w1_words[e].rearrange("s p b -> p s b").bitcast(I32))
+
+        load_w1_scales(0, 2, nc.scalar, nc.vector)
+        load_w1(0)
+        load_w1(1)
+
+        ident = keep.tile([P, P], F32, name="ident", align_bytes=64)
+        make_identity(nc, ident[:])
+
+        xs_planes = {}
+
+        def gather_scales(first, count, queue):
+            got = keep.tile([P, count], U8, name="xs_got%d" % first, align_bytes=64)
+            moved = keep.tile([P, (PASSES - 1) * count], U8, name="xs_moved%d" % first, align_bytes=64)
+            nc.vector.memset(moved[:].bitcast(I32), 0)
+            nc.vector.tensor_copy(got[:], xs_window[:].indirect(offs_sb[:, first // 16 : (first + count) // 16]))
+            for a in range(1, PASSES):
+                queue.dma_start(
+                    moved[0:SHIFT_ROWS, (a - 1) * count : a * count].bitcast(I32),
+                    got[4 * a : 4 * a + SHIFT_ROWS, :].bitcast(I32),
+                )
+            for j in range(first // P, (first + count) // P):
+                col = j * P - first
+                xs_planes[j, 0] = got[:, col : col + P]
+                for a in range(1, PASSES):
+                    xs_planes[j, a] = moved[:, (a - 1) * count + col : (a - 1) * count + col + P]
+
+        xg = {}
+
+        def gather_words(e):
+            for a in range(PASSES):
+                tile = ring.tile([P, C], U32, name="xg%d" % a, align_bytes=64)
+                window = xw[:, a * T : (a + 1) * T].bitcast(U32)
+                nc.vector.tensor_copy(tile[:], window.indirect(offs_sb[:, e * C // 16 : (e + 1) * C // 16]))
+                xg[e, a] = tile
+
+        acc = {}
+
+        def first_pass(j, a):
+            e, b = divmod(j, 2)
+            if a == 0:
+                acc[j] = bank(3 * (e % 2) + b, [P, H])
+            nc.tensor.matmul_mx(
+                out=acc[j][:],
+                lhsT=xg[e, a][:, b * P : (b + 1) * P].bitcast(FP8X4),
+                lhsT_scale=xs_planes[j, a],
+                rhs=w1_sb[e][:, a * 2 * H : (a + 1) * 2 * H].bitcast(FP4X4),
+                rhs_scale=w1_planes[e][:, a * H : (a + 1) * H],
+                start=(a == 0),
+                stop=(a == PASSES - 1),
+            )
+
+        relu = {}
+
+        def relu_block(j):
+            relu[j] = work.tile([P, 4, P], F32, name="relu", align_bytes=64)
+            src = acc[j][:].rearrange("s (p t) -> s t p", t=4)
+            if j >= BLOCKS - 2:
+                nc.vector.tensor_scalar(relu[j][:], src, 0.0, None, ALU.max)
+            else:
+                nc.scalar.activation(relu[j][:], src, ACT.Relu)
+
+        def first_layer(j):
+            for a in range(PASSES):
+                first_pass(j, a)
+            relu_block(j)
+
+        hidden = {}
+
+        def turn_and_square(j, index):
+            e, b = divmod(j, 2)
+            turned = bank(index, [P, 4, P])
+            for t in range(4):
+                nc.tensor.transpose(turned[:, t, :], relu[j][:, t, :], ident[:])
+            if b == 0:
+                hidden[e] = work.tile([P, C, 4], BF16, name="hidden", align_bytes=64)
+            nc.scalar.activation(
+                hidden[e][:, b * P : (b + 1) * P, :], turned[:].rearrange("p t s -> p s t"), ACT.Square
+            )
+
+        hq = {}
+
+        def quantize(first, count):
+            e, col = divmod(first, C)
+            codes = work.tile([P, count], U32, name="h_codes", align_bytes=64)
+            scales = work.tile([P, count], U8, name="h_scales", align_bytes=64)
+            nc.vector.quantize_mx(
+                out=codes[:].bitcast(FP8X4),
+                scales=scales[:],
+                in_=hidden[e][:, col : col + count, :].rearrange("p s t -> p (s t)"),
+            )
+            hq[first] = (codes, scales)
+
+        w2_sb = keep.tile([P, E * W2_BYTES], U8, name="w2_sb", align_bytes=64)
+        y_sb = [keep.tile([P, S], F32, name="y%d" % nb, align_bytes=64) for nb in range(2)]
+
+        w2_planes = keep.tile([P, E * N], U8, name="w2_planes", align_bytes=64)
+
+        def second_product(first, nb, dst):
+            e = first // C
+            codes, scales = hq[first]
+            wcol = e * W2_BYTES + nb * 2 * P
+            nc.tensor.matmul_mx(
+                out=dst,
+                lhsT=w2_sb[:, wcol : wcol + 2 * P].bitcast(FP4X4),
+                lhsT_scale=w2_planes[:, e * N + nb * P : e * N + (nb + 1) * P],
+                rhs=codes[:].bitcast(FP8X4),
+                rhs_scale=scales[:],
+                start=True,
+                stop=True,
+            )
+
+        def second_layer(e, index):
+            y_bank = bank(index, [P, 2, C])
+            for nb in range(2):
+                second_product(e * C, nb, y_bank[:, nb, :])
+            for nb in range(2):
+                nc.scalar.copy(y_sb[nb][:, e * C : (e + 1) * C], y_bank[:, nb, :])
+
+        def second_rows(nb, first, count, index, copy):
+            y_bank = bank(index, [P, 2, count])
+            for i in range(2):
+                second_product(first + i * count, nb, y_bank[:, i, :])
+            copy(y_sb[nb][:, first : first + 2 * count], y_bank[:].rearrange("p i c -> p (i c)"))
+
+        gather_scales(0, FIRST_SLOTS, nc.scalar)
+        gather_words(0)
+        gather_scales(FIRST_SLOTS, S - FIRST_SLOTS, nc.sync)
+        gather_words(1)
+        load_w1_scales(2, E, nc.sync, nc.gpsimd)
+        load_w1(2)
+        nc.gpsimd.memset(w2_planes[:].bitcast(I32), 0)
+        w2s_src = w2_scales.rearrange("e s (q r) n -> r q (e s) n", r=4)
+        for r in range(4):
+            dst = w2_planes[r:P:32, :].bitcast(I32).rearrange("q (e n) -> q e n", e=E)
+            nc.gpsimd.dma_start(dst, w2s_src[r].bitcast(I32))
+        nc.sync.dma_start(
+            w2_sb[:].bitcast(I32).rearrange("p (e b) -> p e b", e=E),
+            w2_words.rearrange("e s p b -> p (e s) b").bitcast(I32),
+        )
+        for e in range(3, E):
+            load_w1(e)
+
+        for e in range(E - 1):
+            banks = 3 * (e % 2)
+            if e < 2:
+                for a in range(PASSES):
+                    first_pass(2 * e, a)
+                    first_pass(2 * e + 1, a)
+                relu_block(2 * e)
+                relu_block(2 * e + 1)
+            else:
+                first_layer(2 * e)
+                first_layer(2 * e + 1)
+            if e + 2 < E:
+                gather_words(e + 2)
+            if e >= 1:
+                turn_and_square(2 * e - 1, banks)
+                quantize((e - 1) * C, C)
+            turn_and_square(2 * e, banks + 2)
+            if e == E - 2:
+                turn_and_square(2 * e + 1, 6)
+                quantize(e * C, C)
+            if e >= 2:
+                second_layer(e - 2, banks + 1)
+
+        gate_sb = keep.tile([P, 2, T], F32, name="gate_sb", align_bytes=64)
+        nc.sync.dma_start(gate_sb[:], gate[:, 0:P, :].rearrange("r p t -> p r t"))
+        for r, pos in enumerate((pos1, pos2)):
+            nc.sync.dma_start(pos_sb[r][:], pos)
+
+        first_layer(BLOCKS - 2)
+        first_layer(BLOCKS - 1)
+        turn_and_square(BLOCKS - 2, 2)
+        quantize(S - 2 * P, P)
+        turn_and_square(BLOCKS - 1, 7)
+        quantize(S - P, P)
+        second_rows(0, (E - 3) * C, C, 1, nc.scalar.copy)
+        second_rows(0, S - C, P, 0, nc.vector.tensor_copy)
+        second_rows(1, (E - 3) * C, C, 2, nc.scalar.copy)
+        second_rows(1, S - C, P, 3, nc.scalar.copy)
+
+        def gated(nb, r, first, count):
+            part = keep.tile([P, count], F32, name="part%d_%d_%d" % (nb, r, first), align_bytes=64)
+            picked = y_sb[nb][:].indirect(pos_sb[r][:, first // 16 : (first + count) // 16])
+            nc.vector.tensor_tensor(part[:], picked, gate_sb[:, r, first : first + count], ALU.mult)
+            return part
+
+        def add_and_store(nb, first, left, right, queue):
+            count = right.shape[1]
+            total = keep.tile([P, count], F32, name="total%d_%d" % (nb, first), align_bytes=64)
+            nc.vector.tensor_tensor(total[:], left, right, ALU.add)
+            queue.dma_start(out[nb * P : (nb + 1) * P, first : first + count], total[:])
+
+        half = T // 2
+        a0 = gated(0, 0, 0, T)
+        b0 = gated(0, 1, 0, T)
+        a1 = gated(1, 0, 0, T)
+        add_and_store(0, 0, a0[:], b0[:], nc.sync)
+        b1 = [gated(1, 1, first, half) for first in (0, half)]
+        add_and_store(1, 0, a1[:, 0:half], b1[0][:], nc.sync)
+        add_and_store(1, half, a1[:, half:T], b1[1][:], nc.scalar)

@@ -37,7 +37,7 @@ def tile_moe_pkd_mlp_relu2_kernel(
         lists = ctx.enter_context(tc.tile_pool(name="lists", bufs=1))
         keep = ctx.enter_context(tc.tile_pool(name="keep", bufs=1))
         ring = ctx.enter_context(tc.tile_pool(name="ring", bufs=2))
-        work = ctx.enter_context(tc.tile_pool(name="work", bufs=4))
+        work = ctx.enter_context(tc.tile_pool(name="work", bufs=5))
         psum = ctx.enter_context(tc.psum_pool(name="psum", bufs=1))
 
         def bank(index, shape):
@@ -64,15 +64,15 @@ def tile_moe_pkd_mlp_relu2_kernel(
 
         w1_planes = {}
 
-        def load_w1_scales(e0, e1, queue, zeroing):
+        def load_w1_scales(e0, e1):
             planes = keep.tile([P, (e1 - e0) * W1_SCALE_BYTES], U8, name="w1_planes%d" % e0, align_bytes=64)
-            zeroing.memset(planes[:].bitcast(I32), 0)
+            nc.vector.memset(planes[:].bitcast(I32), 0)
             for e in range(e0, e1):
                 w1_planes[e] = planes[:, (e - e0) * W1_SCALE_BYTES : (e - e0 + 1) * W1_SCALE_BYTES]
             src = w1_scales[e0:e1].rearrange("e s (q r) i -> r q (e s) i", r=4)
             for r in range(4):
                 dst = planes[r:P:32, :].bitcast(I32).rearrange("q (g i) -> q g i", i=H // 4)
-                queue.dma_start(dst, src[r].bitcast(I32))
+                nc.sync.dma_start(dst, src[r].bitcast(I32))
 
         w1_sb = [keep.tile([P, W1_BYTES], U8, name="w1_%d" % i, align_bytes=64) for i in range(E)]
 
@@ -80,8 +80,8 @@ def tile_moe_pkd_mlp_relu2_kernel(
             dst = w1_sb[e][:].bitcast(I32).rearrange("p (s b) -> p s b", s=PASSES)
             nc.sync.dma_start(dst, w1_words[e].rearrange("s p b -> p s b").bitcast(I32))
 
-        load_w1_scales(0, 2, nc.scalar, nc.vector)
         load_w1(0)
+        load_w1_scales(0, 2)
         load_w1(1)
 
         ident = keep.tile([P, P], F32, name="ident", align_bytes=64)
@@ -152,7 +152,7 @@ def tile_moe_pkd_mlp_relu2_kernel(
             turned = bank(index, [P, 4, P])
             for t in range(4):
                 nc.tensor.transpose(turned[:, t, :], relu[j][:, t, :], ident[:])
-            if b == 0:
+            if e not in hidden:
                 hidden[e] = work.tile([P, C, 4], BF16, name="hidden", align_bytes=64)
             nc.scalar.activation(
                 hidden[e][:, b * P : (b + 1) * P, :], turned[:].rearrange("p t s -> p s t"), ACT.Square
@@ -207,13 +207,13 @@ def tile_moe_pkd_mlp_relu2_kernel(
         gather_words(0)
         gather_scales(FIRST_SLOTS, S - FIRST_SLOTS, nc.sync)
         gather_words(1)
-        load_w1_scales(2, E, nc.sync, nc.gpsimd)
+        load_w1_scales(2, E)
         load_w1(2)
-        nc.gpsimd.memset(w2_planes[:].bitcast(I32), 0)
+        nc.vector.memset(w2_planes[:].bitcast(I32), 0)
         w2s_src = w2_scales.rearrange("e s (q r) n -> r q (e s) n", r=4)
         for r in range(4):
             dst = w2_planes[r:P:32, :].bitcast(I32).rearrange("q (e n) -> q e n", e=E)
-            nc.gpsimd.dma_start(dst, w2s_src[r].bitcast(I32))
+            nc.sync.dma_start(dst, w2s_src[r].bitcast(I32))
         nc.sync.dma_start(
             w2_sb[:].bitcast(I32).rearrange("p (e b) -> p e b", e=E),
             w2_words.rearrange("e s p b -> p (e s) b").bitcast(I32),
@@ -234,10 +234,15 @@ def tile_moe_pkd_mlp_relu2_kernel(
                 first_layer(2 * e + 1)
             if e + 2 < E:
                 gather_words(e + 2)
-            if e >= 1:
+            if e == 1:
+                turn_and_square(0, banks)
+                turn_and_square(2, banks + 2)
+                turn_and_square(1, banks + 1)
+                quantize(0, C)
+            if e >= 2:
                 turn_and_square(2 * e - 1, banks)
                 quantize((e - 1) * C, C)
-            turn_and_square(2 * e, banks + 2)
+                turn_and_square(2 * e, banks + 2)
             if e == E - 2:
                 turn_and_square(2 * e + 1, 6)
                 quantize(e * C, C)

@@ -27,6 +27,7 @@ W2_BYTES = 2 * N
 SCALE_WINDOW = 1024
 FIRST_SLOTS = 2 * C
 SHIFT_ROWS = 112
+WARM_PASSES = 6
 
 
 def tile_moe_pkd_mlp_relu2_kernel(
@@ -37,7 +38,7 @@ def tile_moe_pkd_mlp_relu2_kernel(
         lists = ctx.enter_context(tc.tile_pool(name="lists", bufs=1))
         keep = ctx.enter_context(tc.tile_pool(name="keep", bufs=1))
         ring = ctx.enter_context(tc.tile_pool(name="ring", bufs=2))
-        work = ctx.enter_context(tc.tile_pool(name="work", bufs=5))
+        work = ctx.enter_context(tc.tile_pool(name="work", bufs=6))
         psum = ctx.enter_context(tc.psum_pool(name="psum", bufs=1))
 
         def bank(index, shape):
@@ -48,7 +49,7 @@ def tile_moe_pkd_mlp_relu2_kernel(
         nc.sync.dma_start(offs_sb[:], offs)
 
         xs_window = keep.tile([P, SCALE_WINDOW], U8, name="xs_window", align_bytes=64)
-        nc.vector.memset(xs_window[:].bitcast(I32), 0)
+        nc.gpsimd.memset(xs_window[:].bitcast(I32), 0)
 
         for q in range(4):
             queue = nc.sync if q < 2 else nc.scalar
@@ -57,16 +58,20 @@ def tile_moe_pkd_mlp_relu2_kernel(
                 x_scales[:, 4 * q : 4 * q + 4, :].bitcast(I32),
             )
         xw = keep.tile([P, PASSES * T], I32, name="xw", align_bytes=64)
-        nc.sync.dma_start(
-            xw[:].rearrange("p (a t) -> p a t", a=PASSES),
-            x_words.rearrange("a p t r -> p a (t r)").bitcast(I32),
-        )
+
+        def load_tokens(a0):
+            nc.sync.dma_start(
+                xw[:, a0 * T : (a0 + 2) * T].rearrange("p (a t) -> p a t", a=2),
+                x_words[a0 : a0 + 2].rearrange("a p t r -> p a (t r)").bitcast(I32),
+            )
+
+        load_tokens(0)
 
         w1_planes = {}
 
-        def load_w1_scales(e0, e1):
+        def load_w1_scales(e0, e1, zeroing):
             planes = keep.tile([P, (e1 - e0) * W1_SCALE_BYTES], U8, name="w1_planes%d" % e0, align_bytes=64)
-            nc.vector.memset(planes[:].bitcast(I32), 0)
+            zeroing.memset(planes[:].bitcast(I32), 0)
             for e in range(e0, e1):
                 w1_planes[e] = planes[:, (e - e0) * W1_SCALE_BYTES : (e - e0 + 1) * W1_SCALE_BYTES]
             src = w1_scales[e0:e1].rearrange("e s (q r) i -> r q (e s) i", r=4)
@@ -81,24 +86,26 @@ def tile_moe_pkd_mlp_relu2_kernel(
             nc.sync.dma_start(dst, w1_words[e].rearrange("s p b -> p s b").bitcast(I32))
 
         load_w1(0)
-        load_w1_scales(0, 2)
+        load_tokens(2)
+        load_w1_scales(0, 2, nc.vector)
         load_w1(1)
 
         ident = keep.tile([P, P], F32, name="ident", align_bytes=64)
-        make_identity(nc, ident[:])
 
         xs_planes = {}
+        xs_got = {}
 
-        def gather_scales(first, count, queue):
+        def gather_scales(first, count, queue, zeroing):
             got = keep.tile([P, count], U8, name="xs_got%d" % first, align_bytes=64)
             moved = keep.tile([P, (PASSES - 1) * count], U8, name="xs_moved%d" % first, align_bytes=64)
-            nc.vector.memset(moved[:].bitcast(I32), 0)
+            zeroing.memset(moved[:].bitcast(I32), 0)
             nc.vector.tensor_copy(got[:], xs_window[:].indirect(offs_sb[:, first // 16 : (first + count) // 16]))
             for a in range(1, PASSES):
                 queue.dma_start(
                     moved[0:SHIFT_ROWS, (a - 1) * count : a * count].bitcast(I32),
                     got[4 * a : 4 * a + SHIFT_ROWS, :].bitcast(I32),
                 )
+            xs_got[first] = got
             for j in range(first // P, (first + count) // P):
                 col = j * P - first
                 xs_planes[j, 0] = got[:, col : col + P]
@@ -110,7 +117,8 @@ def tile_moe_pkd_mlp_relu2_kernel(
         def gather_words(e):
             for a in range(PASSES):
                 tile = ring.tile([P, C], U32, name="xg%d" % a, align_bytes=64)
-                window = xw[:, a * T : (a + 1) * T].bitcast(U32)
+                last = max((a + 1) * T, 2 * T + P) if e == 1 else (a + 1) * T
+                window = xw[:, a * T : last].bitcast(U32)
                 nc.vector.tensor_copy(tile[:], window.indirect(offs_sb[:, e * C // 16 : (e + 1) * C // 16]))
                 xg[e, a] = tile
 
@@ -190,26 +198,35 @@ def tile_moe_pkd_mlp_relu2_kernel(
                 stop=True,
             )
 
-        def second_layer(e, index):
-            y_bank = bank(index, [P, 2, C])
-            for nb in range(2):
-                second_product(e * C, nb, y_bank[:, nb, :])
-            for nb in range(2):
-                nc.scalar.copy(y_sb[nb][:, e * C : (e + 1) * C], y_bank[:, nb, :])
-
         def second_rows(nb, first, count, index, copy):
             y_bank = bank(index, [P, 2, count])
             for i in range(2):
                 second_product(first + i * count, nb, y_bank[:, i, :])
             copy(y_sb[nb][:, first : first + 2 * count], y_bank[:].rearrange("p i c -> p (i c)"))
 
-        gather_scales(0, FIRST_SLOTS, nc.scalar)
+        gather_scales(0, FIRST_SLOTS, nc.scalar, nc.vector)
+        zeros = keep.tile([P, 2 * H], BF16, name="zeros", align_bytes=64)
+        nc.gpsimd.memset(zeros[:].bitcast(I32), 0)
+        zero_codes = keep.tile([P, H // 2], U32, name="zero_codes", align_bytes=64)
+        zero_scales = keep.tile([P, H // 2], U8, name="zero_scales", align_bytes=64)
+        nc.vector.quantize_mx(out=zero_codes[:].bitcast(FP8X4), scales=zero_scales[:], in_=zeros[:])
+        warm = bank(7, [P, H])
+        for step in range(WARM_PASSES):
+            nc.tensor.matmul_mx(
+                out=warm[:],
+                lhsT=zero_codes[:, 0:P].bitcast(FP8X4),
+                lhsT_scale=zero_scales[:, 0:P],
+                rhs=zero_codes[:].bitcast(FP4X4),
+                rhs_scale=xs_got[0][:],
+                start=True,
+                stop=True,
+            )
         gather_words(0)
-        gather_scales(FIRST_SLOTS, S - FIRST_SLOTS, nc.sync)
+        gather_scales(FIRST_SLOTS, S - FIRST_SLOTS, nc.sync, nc.gpsimd)
         gather_words(1)
-        load_w1_scales(2, E)
+        load_w1_scales(2, E, nc.gpsimd)
         load_w1(2)
-        nc.vector.memset(w2_planes[:].bitcast(I32), 0)
+        nc.gpsimd.memset(w2_planes[:].bitcast(I32), 0)
         w2s_src = w2_scales.rearrange("e s (q r) n -> r q (e s) n", r=4)
         for r in range(4):
             dst = w2_planes[r:P:32, :].bitcast(I32).rearrange("q (e n) -> q e n", e=E)
@@ -218,12 +235,13 @@ def tile_moe_pkd_mlp_relu2_kernel(
             w2_sb[:].bitcast(I32).rearrange("p (e b) -> p e b", e=E),
             w2_words.rearrange("e s p b -> p (e s) b").bitcast(I32),
         )
+        make_identity(nc, ident[:])
         for e in range(3, E):
             load_w1(e)
 
         for e in range(E - 1):
             banks = 3 * (e % 2)
-            if e < 2:
+            if e == 0:
                 for a in range(PASSES):
                     first_pass(2 * e, a)
                     first_pass(2 * e + 1, a)
@@ -246,23 +264,27 @@ def tile_moe_pkd_mlp_relu2_kernel(
             if e == E - 2:
                 turn_and_square(2 * e + 1, 6)
                 quantize(e * C, C)
-            if e >= 2:
-                second_layer(e - 2, banks + 1)
 
         gate_sb = keep.tile([P, 2, T], F32, name="gate_sb", align_bytes=64)
         nc.sync.dma_start(gate_sb[:], gate[:, 0:P, :].rearrange("r p t -> p r t"))
         for r, pos in enumerate((pos1, pos2)):
             nc.sync.dma_start(pos_sb[r][:], pos)
+        gate_cols = [keep.tile([P, T // P], F32, name="gate_cols%d" % r, align_bytes=64) for r in range(2)]
+        with nc.allow_non_contiguous_dma(reason="one gate value a token and partition"):
+            for r in range(2):
+                nc.sync.dma_start(gate_cols[r][:], gate[r, 0, :].rearrange("(c p) -> p c", p=P))
 
         first_layer(BLOCKS - 2)
         first_layer(BLOCKS - 1)
+        second_rows(0, 0, C, 0, nc.vector.tensor_copy)
         turn_and_square(BLOCKS - 2, 2)
         quantize(S - 2 * P, P)
         turn_and_square(BLOCKS - 1, 7)
         quantize(S - P, P)
-        second_rows(0, (E - 3) * C, C, 1, nc.scalar.copy)
-        second_rows(0, S - C, P, 0, nc.vector.tensor_copy)
-        second_rows(1, (E - 3) * C, C, 2, nc.scalar.copy)
+        second_rows(0, 2 * C, C, 1, nc.scalar.copy)
+        second_rows(0, S - C, P, 6, nc.vector.tensor_copy)
+        second_rows(1, 0, C, 2, nc.scalar.copy)
+        second_rows(1, 2 * C, C, 7, nc.scalar.copy)
         second_rows(1, S - C, P, 3, nc.scalar.copy)
 
         def gated(nb, r, first, count):
@@ -278,10 +300,33 @@ def tile_moe_pkd_mlp_relu2_kernel(
             queue.dma_start(out[nb * P : (nb + 1) * P, first : first + count], total[:])
 
         half = T // 2
-        a0 = gated(0, 0, 0, T)
-        b0 = gated(0, 1, 0, T)
+        groups = ((0, 4), (4, 1))
+        scaled = []
+        for r in range(2):
+            picked = keep.tile([P, T], F32, name="picked%d" % r, align_bytes=64)
+            nc.vector.tensor_copy(picked[:], y_sb[0][:].indirect(pos_sb[r][:]))
+            by_token = keep.tile([P, T // P, P], F32, name="by_token%d" % r, align_bytes=64)
+            for g, (c0, n) in enumerate(groups):
+                turned = bank(4 + 2 * r + g, [P, n, P])
+                for i in range(n):
+                    nc.tensor.transpose(turned[:, i, :], picked[:, (c0 + i) * P : (c0 + i + 1) * P], ident[:])
+                for i in range(n):
+                    nc.scalar.activation(
+                        by_token[:, c0 + i, :], turned[:, i, :], ACT.Copy, scale=gate_cols[r][:, c0 + i : c0 + i + 1]
+                    )
+            scaled.append(by_token)
+        total0 = keep.tile([P, T], F32, name="total0", align_bytes=64)
+        for g, (c0, n) in enumerate(groups):
+            summed = bank(g, [P, n, P])
+            for i in range(n):
+                for r in range(2):
+                    nc.tensor.matmul(
+                        summed[:, i, :], scaled[r][:, c0 + i, :], ident[:], start=(r == 0), stop=(r == 1), is_transpose=True
+                    )
+            cols = slice(c0 * P, (c0 + n) * P)
+            nc.scalar.copy(total0[:, cols], summed[:].rearrange("p i t -> p (i t)"))
+            nc.scalar.dma_start(out[0:P, cols], total0[:, cols])
         a1 = gated(1, 0, 0, T)
-        add_and_store(0, 0, a0[:], b0[:], nc.sync)
         b1 = [gated(1, 1, first, half) for first in (0, half)]
         add_and_store(1, 0, a1[:, 0:half], b1[0][:], nc.sync)
-        add_and_store(1, half, a1[:, half:T], b1[1][:], nc.scalar)
+        add_and_store(1, half, a1[:, half:T], b1[1][:], nc.sync)

@@ -18,16 +18,18 @@ ACT = mybir.ActivationFunctionType
 ALU = mybir.AluOpType
 
 P = 128
+PER_COLUMN = 16
 PASSES = K // 512
 S = E * C
 BLOCKS = S // P
 W1_BYTES = PASSES * 2 * H
 W1_SCALE_BYTES = PASSES * H
 W2_BYTES = 2 * N
+EARLY_EXPERTS = 2
+EARLY_SLOTS = EARLY_EXPERTS * C
 SCALE_WINDOW = 1024
-FIRST_SLOTS = 2 * C
-SHIFT_ROWS = 112
-WARM_PASSES = 6
+MOVED_ROWS = 112
+TOKEN_GROUPS = ((0, 3), (3, 2))
 
 
 def tile_moe_pkd_mlp_relu2_kernel(
@@ -37,20 +39,21 @@ def tile_moe_pkd_mlp_relu2_kernel(
     with ExitStack() as ctx:
         lists = ctx.enter_context(tc.tile_pool(name="lists", bufs=1))
         keep = ctx.enter_context(tc.tile_pool(name="keep", bufs=1))
-        ring = ctx.enter_context(tc.tile_pool(name="ring", bufs=2))
         work = ctx.enter_context(tc.tile_pool(name="work", bufs=6))
         psum = ctx.enter_context(tc.psum_pool(name="psum", bufs=1))
 
         def bank(index, shape):
             return psum.tile(shape, F32, name="bank%d" % index)
 
-        offs_sb = lists.tile([P, S // 16], U16, name="offs_sb")
-        pos_sb = [lists.tile([P, T // 16], U16, name="pos%d_sb" % r) for r in range(2)]
+        def entries(list_sb, first, count):
+            return list_sb[:, first // PER_COLUMN : (first + count) // PER_COLUMN]
+
+        offs_sb = lists.tile([P, S // PER_COLUMN], U16, name="offs_sb")
+        pos_sb = [lists.tile([P, T // PER_COLUMN], U16, name="pos%d_sb" % r) for r in range(2)]
         nc.sync.dma_start(offs_sb[:], offs)
 
         xs_window = keep.tile([P, SCALE_WINDOW], U8, name="xs_window", align_bytes=64)
-        nc.gpsimd.memset(xs_window[:].bitcast(I32), 0)
-
+        nc.vector.memset(xs_window[:].bitcast(I32), 0)
         for q in range(4):
             queue = nc.sync if q < 2 else nc.scalar
             queue.dma_start(
@@ -58,54 +61,53 @@ def tile_moe_pkd_mlp_relu2_kernel(
                 x_scales[:, 4 * q : 4 * q + 4, :].bitcast(I32),
             )
         xw = keep.tile([P, PASSES * T], I32, name="xw", align_bytes=64)
+        nc.sync.dma_start(
+            xw[:].rearrange("p (a t) -> p a t", a=PASSES),
+            x_words.rearrange("a p t r -> p a (t r)").bitcast(I32),
+        )
 
-        def load_tokens(a0):
-            nc.sync.dma_start(
-                xw[:, a0 * T : (a0 + 2) * T].rearrange("p (a t) -> p a t", a=2),
-                x_words[a0 : a0 + 2].rearrange("a p t r -> p a (t r)").bitcast(I32),
-            )
-
-        load_tokens(0)
+        def load_scale_planes(planes, scales):
+            width = scales.shape[3]
+            nc.vector.memset(planes[:].bitcast(I32), 0)
+            rows = scales.rearrange("e a (q r) c -> r q (e a) c", r=4)
+            for r in range(4):
+                dst = planes[r:P:32, :].bitcast(I32).rearrange("q (g c) -> q g c", c=width // 4)
+                nc.sync.dma_start(dst, rows[r].bitcast(I32))
 
         w1_planes = {}
 
-        def load_w1_scales(e0, e1, zeroing):
+        def load_w1_scales(e0, e1):
             planes = keep.tile([P, (e1 - e0) * W1_SCALE_BYTES], U8, name="w1_planes%d" % e0, align_bytes=64)
-            zeroing.memset(planes[:].bitcast(I32), 0)
+            load_scale_planes(planes, w1_scales[e0:e1])
             for e in range(e0, e1):
                 w1_planes[e] = planes[:, (e - e0) * W1_SCALE_BYTES : (e - e0 + 1) * W1_SCALE_BYTES]
-            src = w1_scales[e0:e1].rearrange("e s (q r) i -> r q (e s) i", r=4)
-            for r in range(4):
-                dst = planes[r:P:32, :].bitcast(I32).rearrange("q (g i) -> q g i", i=H // 4)
-                nc.sync.dma_start(dst, src[r].bitcast(I32))
 
-        w1_sb = [keep.tile([P, W1_BYTES], U8, name="w1_%d" % i, align_bytes=64) for i in range(E)]
+        w1_sb = [keep.tile([P, W1_BYTES], U8, name="w1_%d" % e, align_bytes=64) for e in range(E)]
 
         def load_w1(e):
-            dst = w1_sb[e][:].bitcast(I32).rearrange("p (s b) -> p s b", s=PASSES)
-            nc.sync.dma_start(dst, w1_words[e].rearrange("s p b -> p s b").bitcast(I32))
+            dst = w1_sb[e][:].bitcast(I32).rearrange("p (a b) -> p a b", a=PASSES)
+            nc.sync.dma_start(dst, w1_words[e].rearrange("a p b -> p a b").bitcast(I32))
 
         load_w1(0)
-        load_tokens(2)
-        load_w1_scales(0, 2, nc.vector)
+        load_w1_scales(0, EARLY_EXPERTS)
         load_w1(1)
+        load_w1(2)
 
         ident = keep.tile([P, P], F32, name="ident", align_bytes=64)
+        make_identity(nc, ident[:])
 
         xs_planes = {}
-        xs_got = {}
 
-        def gather_scales(first, count, queue, zeroing):
+        def gather_scales(first, count, queue):
             got = keep.tile([P, count], U8, name="xs_got%d" % first, align_bytes=64)
             moved = keep.tile([P, (PASSES - 1) * count], U8, name="xs_moved%d" % first, align_bytes=64)
-            zeroing.memset(moved[:].bitcast(I32), 0)
-            nc.vector.tensor_copy(got[:], xs_window[:].indirect(offs_sb[:, first // 16 : (first + count) // 16]))
+            nc.vector.memset(moved[:].bitcast(I32), 0)
+            nc.vector.tensor_copy(got[:], xs_window[:].indirect(entries(offs_sb, first, count)))
             for a in range(1, PASSES):
                 queue.dma_start(
-                    moved[0:SHIFT_ROWS, (a - 1) * count : a * count].bitcast(I32),
-                    got[4 * a : 4 * a + SHIFT_ROWS, :].bitcast(I32),
+                    moved[0:MOVED_ROWS, (a - 1) * count : a * count].bitcast(I32),
+                    got[4 * a : 4 * a + MOVED_ROWS, :].bitcast(I32),
                 )
-            xs_got[first] = got
             for j in range(first // P, (first + count) // P):
                 col = j * P - first
                 xs_planes[j, 0] = got[:, col : col + P]
@@ -116,18 +118,35 @@ def tile_moe_pkd_mlp_relu2_kernel(
 
         def gather_words(e):
             for a in range(PASSES):
-                tile = ring.tile([P, C], U32, name="xg%d" % a, align_bytes=64)
-                last = max((a + 1) * T, 2 * T + P) if e == 1 else (a + 1) * T
-                window = xw[:, a * T : last].bitcast(U32)
-                nc.vector.tensor_copy(tile[:], window.indirect(offs_sb[:, e * C // 16 : (e + 1) * C // 16]))
-                xg[e, a] = tile
+                xg[e, a] = keep.tile([P, C], U32, name="xg%d_%d" % (e, a), align_bytes=64)
+                window = xw[:, a * T : (a + 1) * T].bitcast(U32)
+                nc.vector.tensor_copy(xg[e, a][:], window.indirect(entries(offs_sb, e * C, C)))
+
+        gather_scales(0, EARLY_SLOTS, nc.scalar)
+        gather_words(0)
+        gather_scales(EARLY_SLOTS, S - EARLY_SLOTS, nc.sync)
+        load_w1_scales(EARLY_EXPERTS, E)
+        for e in range(1, E):
+            gather_words(e)
+        for e in range(3, E):
+            load_w1(e)
+        w2_planes = keep.tile([P, E * N], U8, name="w2_planes", align_bytes=64)
+        load_scale_planes(w2_planes, w2_scales)
+        w2_sb = keep.tile([P, E * W2_BYTES], U8, name="w2_sb", align_bytes=64)
+        nc.sync.dma_start(
+            w2_sb[:].bitcast(I32).rearrange("p (e b) -> p e b", e=E),
+            w2_words.rearrange("e a p b -> p (e a) b").bitcast(I32),
+        )
+
+        def first_bank(e):
+            return 3 * (e % 2)
 
         acc = {}
 
         def first_pass(j, a):
             e, b = divmod(j, 2)
             if a == 0:
-                acc[j] = bank(3 * (e % 2) + b, [P, H])
+                acc[j] = bank(first_bank(e) + b, [P, H])
             nc.tensor.matmul_mx(
                 out=acc[j][:],
                 lhsT=xg[e, a][:, b * P : (b + 1) * P].bitcast(FP8X4),
@@ -143,7 +162,7 @@ def tile_moe_pkd_mlp_relu2_kernel(
         def relu_block(j):
             relu[j] = work.tile([P, 4, P], F32, name="relu", align_bytes=64)
             src = acc[j][:].rearrange("s (p t) -> s t p", t=4)
-            if j >= BLOCKS - 2:
+            if j // 2 == E - 1:
                 nc.vector.tensor_scalar(relu[j][:], src, 0.0, None, ALU.max)
             else:
                 nc.scalar.activation(relu[j][:], src, ACT.Relu)
@@ -166,7 +185,7 @@ def tile_moe_pkd_mlp_relu2_kernel(
                 hidden[e][:, b * P : (b + 1) * P, :], turned[:].rearrange("p t s -> p s t"), ACT.Square
             )
 
-        hq = {}
+        h_mx = {}
 
         def quantize(first, count):
             e, col = divmod(first, C)
@@ -177,93 +196,30 @@ def tile_moe_pkd_mlp_relu2_kernel(
                 scales=scales[:],
                 in_=hidden[e][:, col : col + count, :].rearrange("p s t -> p (s t)"),
             )
-            hq[first] = (codes, scales)
-
-        w2_sb = keep.tile([P, E * W2_BYTES], U8, name="w2_sb", align_bytes=64)
-        y_sb = [keep.tile([P, S], F32, name="y%d" % nb, align_bytes=64) for nb in range(2)]
-
-        w2_planes = keep.tile([P, E * N], U8, name="w2_planes", align_bytes=64)
-
-        def second_product(first, nb, dst):
-            e = first // C
-            codes, scales = hq[first]
-            wcol = e * W2_BYTES + nb * 2 * P
-            nc.tensor.matmul_mx(
-                out=dst,
-                lhsT=w2_sb[:, wcol : wcol + 2 * P].bitcast(FP4X4),
-                lhsT_scale=w2_planes[:, e * N + nb * P : e * N + (nb + 1) * P],
-                rhs=codes[:].bitcast(FP8X4),
-                rhs_scale=scales[:],
-                start=True,
-                stop=True,
-            )
-
-        def second_rows(nb, first, count, index, copy):
-            y_bank = bank(index, [P, 2, count])
-            for i in range(2):
-                second_product(first + i * count, nb, y_bank[:, i, :])
-            copy(y_sb[nb][:, first : first + 2 * count], y_bank[:].rearrange("p i c -> p (i c)"))
-
-        gather_scales(0, FIRST_SLOTS, nc.scalar, nc.vector)
-        zeros = keep.tile([P, 2 * H], BF16, name="zeros", align_bytes=64)
-        nc.gpsimd.memset(zeros[:].bitcast(I32), 0)
-        zero_codes = keep.tile([P, H // 2], U32, name="zero_codes", align_bytes=64)
-        zero_scales = keep.tile([P, H // 2], U8, name="zero_scales", align_bytes=64)
-        nc.vector.quantize_mx(out=zero_codes[:].bitcast(FP8X4), scales=zero_scales[:], in_=zeros[:])
-        warm = bank(7, [P, H])
-        for step in range(WARM_PASSES):
-            nc.tensor.matmul_mx(
-                out=warm[:],
-                lhsT=zero_codes[:, 0:P].bitcast(FP8X4),
-                lhsT_scale=zero_scales[:, 0:P],
-                rhs=zero_codes[:].bitcast(FP4X4),
-                rhs_scale=xs_got[0][:],
-                start=True,
-                stop=True,
-            )
-        gather_words(0)
-        gather_scales(FIRST_SLOTS, S - FIRST_SLOTS, nc.sync, nc.gpsimd)
-        gather_words(1)
-        load_w1_scales(2, E, nc.gpsimd)
-        load_w1(2)
-        nc.gpsimd.memset(w2_planes[:].bitcast(I32), 0)
-        w2s_src = w2_scales.rearrange("e s (q r) n -> r q (e s) n", r=4)
-        for r in range(4):
-            dst = w2_planes[r:P:32, :].bitcast(I32).rearrange("q (e n) -> q e n", e=E)
-            nc.sync.dma_start(dst, w2s_src[r].bitcast(I32))
-        nc.sync.dma_start(
-            w2_sb[:].bitcast(I32).rearrange("p (e b) -> p e b", e=E),
-            w2_words.rearrange("e s p b -> p (e s) b").bitcast(I32),
-        )
-        make_identity(nc, ident[:])
-        for e in range(3, E):
-            load_w1(e)
+            h_mx[first] = (codes, scales)
 
         for e in range(E - 1):
-            banks = 3 * (e % 2)
+            own = first_bank(e)
             if e == 0:
                 for a in range(PASSES):
-                    first_pass(2 * e, a)
-                    first_pass(2 * e + 1, a)
-                relu_block(2 * e)
-                relu_block(2 * e + 1)
+                    first_pass(0, a)
+                    first_pass(1, a)
+                relu_block(0)
+                relu_block(1)
             else:
                 first_layer(2 * e)
                 first_layer(2 * e + 1)
-            if e + 2 < E:
-                gather_words(e + 2)
             if e == 1:
-                turn_and_square(0, banks)
-                turn_and_square(2, banks + 2)
-                turn_and_square(1, banks + 1)
+                turn_and_square(0, own)
+                turn_and_square(2, own + 2)
+                turn_and_square(1, own + 1)
                 quantize(0, C)
             if e >= 2:
-                turn_and_square(2 * e - 1, banks)
+                turn_and_square(2 * e - 1, own)
                 quantize((e - 1) * C, C)
-                turn_and_square(2 * e, banks + 2)
-            if e == E - 2:
-                turn_and_square(2 * e + 1, 6)
-                quantize(e * C, C)
+                turn_and_square(2 * e, own + 2)
+        turn_and_square(BLOCKS - 3, 6)
+        quantize(S - 2 * C, C)
 
         gate_sb = keep.tile([P, 2, T], F32, name="gate_sb", align_bytes=64)
         nc.sync.dma_start(gate_sb[:], gate[:, 0:P, :].rearrange("r p t -> p r t"))
@@ -274,59 +230,73 @@ def tile_moe_pkd_mlp_relu2_kernel(
             for r in range(2):
                 nc.sync.dma_start(gate_cols[r][:], gate[r, 0, :].rearrange("(c p) -> p c", p=P))
 
+        y_sb = [keep.tile([P, S], F32, name="y%d" % nb, align_bytes=64) for nb in range(2)]
+
+        def second_layer(nb, first, count, index, copy):
+            y_bank = bank(index, [P, 2, count])
+            for piece in range(2):
+                slot = first + piece * count
+                e = slot // C
+                codes, scales = h_mx[slot]
+                col = e * N + nb * P
+                nc.tensor.matmul_mx(
+                    out=y_bank[:, piece, :],
+                    lhsT=w2_sb[:, 2 * col : 2 * (col + P)].bitcast(FP4X4),
+                    lhsT_scale=w2_planes[:, col : col + P],
+                    rhs=codes[:].bitcast(FP8X4),
+                    rhs_scale=scales[:],
+                    start=True,
+                    stop=True,
+                )
+            copy(y_sb[nb][:, first : first + 2 * count], y_bank[:].rearrange("p i c -> p (i c)"))
+
         first_layer(BLOCKS - 2)
         first_layer(BLOCKS - 1)
-        second_rows(0, 0, C, 0, nc.vector.tensor_copy)
+        second_layer(0, 0, C, 0, nc.vector.tensor_copy)
         turn_and_square(BLOCKS - 2, 2)
         quantize(S - 2 * P, P)
         turn_and_square(BLOCKS - 1, 7)
         quantize(S - P, P)
-        second_rows(0, 2 * C, C, 1, nc.scalar.copy)
-        second_rows(0, S - C, P, 6, nc.vector.tensor_copy)
-        second_rows(1, 0, C, 2, nc.scalar.copy)
-        second_rows(1, 2 * C, C, 7, nc.scalar.copy)
-        second_rows(1, S - C, P, 3, nc.scalar.copy)
+        second_layer(0, 2 * C, C, 1, nc.scalar.copy)
+        second_layer(0, S - C, P, 6, nc.vector.tensor_copy)
+        second_layer(1, 0, C, 2, nc.scalar.copy)
+        second_layer(1, 2 * C, C, 7, nc.scalar.copy)
+        second_layer(1, S - C, P, 3, nc.scalar.copy)
 
-        def gated(nb, r, first, count):
-            part = keep.tile([P, count], F32, name="part%d_%d_%d" % (nb, r, first), align_bytes=64)
-            picked = y_sb[nb][:].indirect(pos_sb[r][:, first // 16 : (first + count) // 16])
-            nc.vector.tensor_tensor(part[:], picked, gate_sb[:, r, first : first + count], ALU.mult)
-            return part
-
-        def add_and_store(nb, first, left, right, queue):
-            count = right.shape[1]
-            total = keep.tile([P, count], F32, name="total%d_%d" % (nb, first), align_bytes=64)
-            nc.vector.tensor_tensor(total[:], left, right, ALU.add)
-            queue.dma_start(out[nb * P : (nb + 1) * P, first : first + count], total[:])
-
-        half = T // 2
-        groups = ((0, 4), (4, 1))
-        scaled = []
-        for r in range(2):
-            picked = keep.tile([P, T], F32, name="picked%d" % r, align_bytes=64)
-            nc.vector.tensor_copy(picked[:], y_sb[0][:].indirect(pos_sb[r][:]))
-            by_token = keep.tile([P, T // P, P], F32, name="by_token%d" % r, align_bytes=64)
-            for g, (c0, n) in enumerate(groups):
-                turned = bank(4 + 2 * r + g, [P, n, P])
-                for i in range(n):
-                    nc.tensor.transpose(turned[:, i, :], picked[:, (c0 + i) * P : (c0 + i + 1) * P], ident[:])
-                for i in range(n):
-                    nc.scalar.activation(
-                        by_token[:, c0 + i, :], turned[:, i, :], ACT.Copy, scale=gate_cols[r][:, c0 + i : c0 + i + 1]
-                    )
-            scaled.append(by_token)
         total0 = keep.tile([P, T], F32, name="total0", align_bytes=64)
-        for g, (c0, n) in enumerate(groups):
+        for g, (c0, n) in enumerate(TOKEN_GROUPS):
+            scaled = []
+            for r in range(2):
+                picked = keep.tile([P, n * P], F32, name="picked%d_%d" % (r, g), align_bytes=64)
+                nc.vector.tensor_copy(picked[:], y_sb[0][:].indirect(entries(pos_sb[r], c0 * P, n * P)))
+                by_token = bank(4 + 2 * g + r, [P, n, P])
+                for i in range(n):
+                    nc.tensor.transpose(by_token[:, i, :], picked[:, i * P : (i + 1) * P], ident[:])
+                product = keep.tile([P, n, P], F32, name="product%d_%d" % (r, g), align_bytes=64)
+                for i in range(n):
+                    token_gate = gate_cols[r][:, c0 + i : c0 + i + 1]
+                    nc.scalar.activation(product[:, i, :], by_token[:, i, :], ACT.Copy, scale=token_gate)
+                scaled.append(product)
             summed = bank(g, [P, n, P])
             for i in range(n):
                 for r in range(2):
                     nc.tensor.matmul(
-                        summed[:, i, :], scaled[r][:, c0 + i, :], ident[:], start=(r == 0), stop=(r == 1), is_transpose=True
+                        summed[:, i, :], scaled[r][:, i, :], ident[:], start=(r == 0), stop=(r == 1), is_transpose=True
                     )
             cols = slice(c0 * P, (c0 + n) * P)
             nc.scalar.copy(total0[:, cols], summed[:].rearrange("p i t -> p (i t)"))
             nc.scalar.dma_start(out[0:P, cols], total0[:, cols])
-        a1 = gated(1, 0, 0, T)
-        b1 = [gated(1, 1, first, half) for first in (0, half)]
-        add_and_store(1, 0, a1[:, 0:half], b1[0][:], nc.sync)
-        add_and_store(1, half, a1[:, half:T], b1[1][:], nc.sync)
+
+        def gated(r, first, count):
+            part = keep.tile([P, count], F32, name="part%d_%d" % (r, first), align_bytes=64)
+            picked_y = y_sb[1][:].indirect(entries(pos_sb[r], first, count))
+            nc.vector.tensor_tensor(part[:], picked_y, gate_sb[:, r, first : first + count], ALU.mult)
+            return part
+
+        half = T // 2
+        first_choice = gated(0, 0, T)
+        second_choice = [gated(1, first, half) for first in (0, half)]
+        for part, first in zip(second_choice, (0, half)):
+            total1 = keep.tile([P, half], F32, name="total1_%d" % first, align_bytes=64)
+            nc.vector.tensor_tensor(total1[:], first_choice[:, first : first + half], part[:], ALU.add)
+            nc.sync.dma_start(out[P:N, first : first + half], total1[:])

from contextlib import ExitStack

import concourse.mybir as mybir
from concourse.masks import make_identity

K, T, E, C, H, N = 2048, 640, 5, 256, 512, 256
FLOPS = 2 * E * C * (K * H + H * N)

F32 = mybir.dt.float32
BF16 = mybir.dt.bfloat16
I32 = mybir.dt.int32
U32 = mybir.dt.uint32
U16 = mybir.dt.uint16
U8 = mybir.dt.uint8
FP8X4 = mybir.dt.float8_e4m3fn_x4
FP4X4 = mybir.dt.float4_e2m1fn_x4
ACT = mybir.ActivationFunctionType
ALU = mybir.AluOpType

P = 128
PER_COLUMN = 16
PASSES = K // 512
S = E * C
BLOCKS = S // P
W1_BYTES = PASSES * 2 * H
W1_SCALE_BYTES = PASSES * H
W2_BYTES = 2 * N
EARLY_EXPERTS = 2
EARLY_SLOTS = EARLY_EXPERTS * C
SCALE_WINDOW = 1024
MOVED_ROWS = 112
TOKEN_GROUPS = ((0, 3), (3, 2))


def tile_moe_pkd_mlp_relu2_kernel(
    tc, x_words, x_scales, w1_words, w1_scales, w2_words, w2_scales, gate, offs, pos1, pos2, out
):
    nc = tc.nc
    with ExitStack() as ctx:
        lists = ctx.enter_context(tc.tile_pool(name="lists", bufs=1))
        keep = ctx.enter_context(tc.tile_pool(name="keep", bufs=1))
        work = ctx.enter_context(tc.tile_pool(name="work", bufs=6))
        psum = ctx.enter_context(tc.psum_pool(name="psum", bufs=1))

        def bank(index, shape):
            return psum.tile(shape, F32, name="bank%d" % index)

        def entries(list_sb, first, count):
            return list_sb[:, first // PER_COLUMN : (first + count) // PER_COLUMN]

        offs_sb = lists.tile([P, S // PER_COLUMN], U16, name="offs_sb")
        pos_sb = [lists.tile([P, T // PER_COLUMN], U16, name="pos%d_sb" % r) for r in range(2)]
        nc.sync.dma_start(offs_sb[:], offs)

        xs_window = keep.tile([P, SCALE_WINDOW], U8, name="xs_window", align_bytes=64)
        nc.vector.memset(xs_window[:].bitcast(I32), 0)
        for q in range(4):
            queue = nc.sync if q < 2 else nc.scalar
            queue.dma_start(
                xs_window[32 * q : 32 * q + 16, 0:T].bitcast(I32),
                x_scales[:, 4 * q : 4 * q + 4, :].bitcast(I32),
            )
        xw = keep.tile([P, PASSES * T], I32, name="xw", align_bytes=64)
        nc.sync.dma_start(
            xw[:].rearrange("p (a t) -> p a t", a=PASSES),
            x_words.rearrange("a p t r -> p a (t r)").bitcast(I32),
        )

        def load_scale_planes(planes, scales):
            width = scales.shape[3]
            nc.vector.memset(planes[:].bitcast(I32), 0)
            rows = scales.rearrange("e a (q r) c -> r q (e a) c", r=4)
            for r in range(4):
                dst = planes[r:P:32, :].bitcast(I32).rearrange("q (g c) -> q g c", c=width // 4)
                nc.sync.dma_start(dst, rows[r].bitcast(I32))

        w1_planes = {}

        def load_w1_scales(e0, e1):
            planes = keep.tile([P, (e1 - e0) * W1_SCALE_BYTES], U8, name="w1_planes%d" % e0, align_bytes=64)
            load_scale_planes(planes, w1_scales[e0:e1])
            for e in range(e0, e1):
                w1_planes[e] = planes[:, (e - e0) * W1_SCALE_BYTES : (e - e0 + 1) * W1_SCALE_BYTES]

        w1_sb = [keep.tile([P, W1_BYTES], U8, name="w1_%d" % e, align_bytes=64) for e in range(E)]

        def load_w1(e):
            dst = w1_sb[e][:].bitcast(I32).rearrange("p (a b) -> p a b", a=PASSES)
            nc.sync.dma_start(dst, w1_words[e].rearrange("a p b -> p a b").bitcast(I32))

        load_w1(0)
        load_w1_scales(0, EARLY_EXPERTS)
        load_w1(1)
        load_w1(2)

        ident = keep.tile([P, P], F32, name="ident", align_bytes=64)
        make_identity(nc, ident[:])

        xs_planes = {}

        def gather_scales(first, count, queue):
            got = keep.tile([P, count], U8, name="xs_got%d" % first, align_bytes=64)
            moved = keep.tile([P, (PASSES - 1) * count], U8, name="xs_moved%d" % first, align_bytes=64)
            nc.vector.memset(moved[:].bitcast(I32), 0)
            nc.vector.tensor_copy(got[:], xs_window[:].indirect(entries(offs_sb, first, count)))
            for a in range(1, PASSES):
                queue.dma_start(
                    moved[0:MOVED_ROWS, (a - 1) * count : a * count].bitcast(I32),
                    got[4 * a : 4 * a + MOVED_ROWS, :].bitcast(I32),
                )
            for j in range(first // P, (first + count) // P):
                col = j * P - first
                xs_planes[j, 0] = got[:, col : col + P]
                for a in range(1, PASSES):
                    xs_planes[j, a] = moved[:, (a - 1) * count + col : (a - 1) * count + col + P]

        xg = {}

        def gather_words(e):
            for a in range(PASSES):
                xg[e, a] = keep.tile([P, C], U32, name="xg%d_%d" % (e, a), align_bytes=64)
                window = xw[:, a * T : (a + 1) * T].bitcast(U32)
                nc.vector.tensor_copy(xg[e, a][:], window.indirect(entries(offs_sb, e * C, C)))

        gather_scales(0, EARLY_SLOTS, nc.scalar)
        gather_words(0)
        gather_scales(EARLY_SLOTS, S - EARLY_SLOTS, nc.sync)
        load_w1_scales(EARLY_EXPERTS, E)
        for e in range(1, E):
            gather_words(e)
        for e in range(3, E):
            load_w1(e)
        w2_planes = keep.tile([P, E * N], U8, name="w2_planes", align_bytes=64)
        load_scale_planes(w2_planes, w2_scales)
        w2_sb = keep.tile([P, E * W2_BYTES], U8, name="w2_sb", align_bytes=64)
        nc.sync.dma_start(
            w2_sb[:].bitcast(I32).rearrange("p (e b) -> p e b", e=E),
            w2_words.rearrange("e a p b -> p (e a) b").bitcast(I32),
        )

        def first_bank(e):
            return 3 * (e % 2)

        acc = {}

        def first_pass(j, a):
            e, b = divmod(j, 2)
            if a == 0:
                acc[j] = bank(first_bank(e) + b, [P, H])
            nc.tensor.matmul_mx(
                out=acc[j][:],
                lhsT=xg[e, a][:, b * P : (b + 1) * P].bitcast(FP8X4),
                lhsT_scale=xs_planes[j, a],
                rhs=w1_sb[e][:, a * 2 * H : (a + 1) * 2 * H].bitcast(FP4X4),
                rhs_scale=w1_planes[e][:, a * H : (a + 1) * H],
                start=(a == 0),
                stop=(a == PASSES - 1),
            )

        relu = {}

        def relu_block(j):
            relu[j] = work.tile([P, 4, P], F32, name="relu", align_bytes=64)
            src = acc[j][:].rearrange("s (p t) -> s t p", t=4)
            if j // 2 == E - 1:
                nc.vector.tensor_scalar(relu[j][:], src, 0.0, None, ALU.max)
            else:
                nc.scalar.activation(relu[j][:], src, ACT.Relu)

        def first_layer(j):
            for a in range(PASSES):
                first_pass(j, a)
            relu_block(j)

        hidden = {}

        def turn_and_square(j, index):
            e, b = divmod(j, 2)
            turned = bank(index, [P, 4, P])
            for t in range(4):
                nc.tensor.transpose(turned[:, t, :], relu[j][:, t, :], ident[:])
            if e not in hidden:
                hidden[e] = work.tile([P, C, 4], BF16, name="hidden", align_bytes=64)
            nc.scalar.activation(
                hidden[e][:, b * P : (b + 1) * P, :], turned[:].rearrange("p t s -> p s t"), ACT.Square
            )

        h_mx = {}

        def quantize(first, count):
            e, col = divmod(first, C)
            codes = work.tile([P, count], U32, name="h_codes", align_bytes=64)
            scales = work.tile([P, count], U8, name="h_scales", align_bytes=64)
            nc.vector.quantize_mx(
                out=codes[:].bitcast(FP8X4),
                scales=scales[:],
                in_=hidden[e][:, col : col + count, :].rearrange("p s t -> p (s t)"),
            )
            h_mx[first] = (codes, scales)

        for e in range(E - 1):
            own = first_bank(e)
            if e == 0:
                for a in range(PASSES):
                    first_pass(0, a)
                    first_pass(1, a)
                relu_block(0)
                relu_block(1)
            else:
                first_layer(2 * e)
                first_layer(2 * e + 1)
            if e == 1:
                turn_and_square(0, own)
                turn_and_square(2, own + 2)
                turn_and_square(1, own + 1)
                quantize(0, C)
            if e >= 2:
                turn_and_square(2 * e - 1, own)
                quantize((e - 1) * C, C)
                turn_and_square(2 * e, own + 2)
        turn_and_square(BLOCKS - 3, 6)
        quantize(S - 2 * C, C)

        gate_sb = keep.tile([P, 2, T], F32, name="gate_sb", align_bytes=64)
        nc.sync.dma_start(gate_sb[:], gate[:, 0:P, :].rearrange("r p t -> p r t"))
        for r, pos in enumerate((pos1, pos2)):
            nc.sync.dma_start(pos_sb[r][:], pos)
        gate_cols = [keep.tile([P, T // P], F32, name="gate_cols%d" % r, align_bytes=64) for r in range(2)]
        with nc.allow_non_contiguous_dma(reason="one gate value a token and partition"):
            for r in range(2):
                nc.sync.dma_start(gate_cols[r][:], gate[r, 0, :].rearrange("(c p) -> p c", p=P))

        y_sb = [keep.tile([P, S], F32, name="y%d" % nb, align_bytes=64) for nb in range(2)]

        def second_layer(nb, first, count, index, copy):
            y_bank = bank(index, [P, 2, count])
            for piece in range(2):
                slot = first + piece * count
                e = slot // C
                codes, scales = h_mx[slot]
                col = e * N + nb * P
                nc.tensor.matmul_mx(
                    out=y_bank[:, piece, :],
                    lhsT=w2_sb[:, 2 * col : 2 * (col + P)].bitcast(FP4X4),
                    lhsT_scale=w2_planes[:, col : col + P],
                    rhs=codes[:].bitcast(FP8X4),
                    rhs_scale=scales[:],
                    start=True,
                    stop=True,
                )
            copy(y_sb[nb][:, first : first + 2 * count], y_bank[:].rearrange("p i c -> p (i c)"))

        first_layer(BLOCKS - 2)
        first_layer(BLOCKS - 1)
        second_layer(0, 0, C, 0, nc.vector.tensor_copy)
        turn_and_square(BLOCKS - 2, 2)
        quantize(S - 2 * P, P)
        turn_and_square(BLOCKS - 1, 7)
        quantize(S - P, P)
        second_layer(0, 2 * C, C, 1, nc.scalar.copy)
        second_layer(0, S - C, P, 6, nc.vector.tensor_copy)
        second_layer(1, 0, C, 2, nc.scalar.copy)
        second_layer(1, 2 * C, C, 7, nc.scalar.copy)
        second_layer(1, S - C, P, 3, nc.scalar.copy)

        total0 = keep.tile([P, T], F32, name="total0", align_bytes=64)
        for g, (c0, n) in enumerate(TOKEN_GROUPS):
            scaled = []
            for r in range(2):
                picked = keep.tile([P, n * P], F32, name="picked%d_%d" % (r, g), align_bytes=64)
                nc.vector.tensor_copy(picked[:], y_sb[0][:].indirect(entries(pos_sb[r], c0 * P, n * P)))
                by_token = bank(4 + 2 * g + r, [P, n, P])
                for i in range(n):
                    nc.tensor.transpose(by_token[:, i, :], picked[:, i * P : (i + 1) * P], ident[:])
                product = keep.tile([P, n, P], F32, name="product%d_%d" % (r, g), align_bytes=64)
                for i in range(n):
                    token_gate = gate_cols[r][:, c0 + i : c0 + i + 1]
                    nc.scalar.activation(product[:, i, :], by_token[:, i, :], ACT.Copy, scale=token_gate)
                scaled.append(product)
            summed = bank(g, [P, n, P])
            for i in range(n):
                for r in range(2):
                    nc.tensor.matmul(
                        summed[:, i, :], scaled[r][:, i, :], ident[:], start=(r == 0), stop=(r == 1), is_transpose=True
                    )
            cols = slice(c0 * P, (c0 + n) * P)
            nc.scalar.copy(total0[:, cols], summed[:].rearrange("p i t -> p (i t)"))
            nc.scalar.dma_start(out[0:P, cols], total0[:, cols])

        def gated(r, first, count):
            part = keep.tile([P, count], F32, name="part%d_%d" % (r, first), align_bytes=64)
            picked_y = y_sb[1][:].indirect(entries(pos_sb[r], first, count))
            nc.vector.tensor_tensor(part[:], picked_y, gate_sb[:, r, first : first + count], ALU.mult)
            return part

        half = T // 2
        first_choice = gated(0, 0, T)
        second_choice = [gated(1, first, half) for first in (0, half)]
        for part, first in zip(second_choice, (0, half)):
            total1 = keep.tile([P, half], F32, name="total1_%d" % first, align_bytes=64)
            nc.vector.tensor_tensor(total1[:], first_choice[:, first : first + half], part[:], ALU.add)
            nc.sync.dma_start(out[P:N, first : first + half], total1[:])
